import numpy as np
import ml_dtypes


def mxq(x, axis, fmt="e4m3"):
    dtype, down = {"e4m3": (ml_dtypes.float8_e4m3fn, 7), "e5m2": (ml_dtypes.float8_e5m2, 14)}[fmt]
    v = np.moveaxis(np.asarray(x, np.float32).astype(ml_dtypes.bfloat16).astype(np.float64), axis, -1)
    blocks = v.reshape(v.shape[:-1] + (-1, 32))
    amax = np.abs(blocks).max(-1, keepdims=True)
    byte = np.maximum(np.where(amax > 0, np.frexp(amax)[1] - 1 + 127, 0) - down, 1)
    scale = np.exp2(byte - 127.0)
    codes = (blocks / scale).astype(np.float32).astype(dtype).astype(np.float64)
    return np.moveaxis((codes * scale).reshape(v.shape), -1, axis)


WIDE = False


def mx_kscale(k):
    if not WIDE:
        return np.ones(k)
    levels = np.array([10, -10, 5, -5, 0])
    if k % 512:
        return np.exp2(np.random.permutation(np.resize(levels, k // 32))).repeat(32)
    a = np.empty((k // 512, 16))
    for p in range(k // 512):
        a[p, :8] = np.random.permutation(np.resize(levels, 8))
        for g in range(8):
            far = levels[np.abs(levels - a[p, g]) >= 10]
            a[p, g + 8] = far[np.random.randint(len(far))]
    return np.exp2(a.ravel()).repeat(32)


def f64(x):
    return np.asarray(x).astype(np.float64)


def striped(idx):
    return np.tile(idx.reshape(-1, 16).T, (8, 1)).astype(np.uint16)


def unstriped(offs):
    return offs[:16].T.reshape(-1).astype(np.int64)


E2M1 = np.array([0.0, 0.5, 1.0, 1.5, 2.0, 3.0, 4.0, 6.0, -0.0, -0.5, -1.0, -1.5, -2.0, -3.0, -4.0, -6.0])


def pack_weight(w, fmt):
    k, n = w.shape
    w = f64(np.asarray(w, np.float32).astype(ml_dtypes.bfloat16)).reshape(k // 32, 32, n)
    amax = np.abs(w).max(1)
    if fmt == "e4m3":
        byte = np.frexp(amax)[1] - 1 + 127 - 7
    else:
        mant, ex = np.frexp(amax / 6.0)
        byte = np.where(mant > 0.5, ex, ex - 1) + 127
    byte = np.clip(np.where(amax > 0, byte, 1), 1, 254)
    scaled = (w * np.exp2(127.0 - byte)[:, None, :]).reshape(k, n).astype(np.float32)
    by_word = np.ascontiguousarray(scaled.reshape(k // 512, 128, 4, n).transpose(0, 1, 3, 2))
    if fmt == "e4m3":
        words = by_word.astype(ml_dtypes.float8_e4m3fn).view(np.uint8)
    else:
        c = by_word.astype(ml_dtypes.float4_e2m1fn).view(np.uint8) & 0xF
        words = (c[..., 0::2] | (c[..., 1::2] << 4)).reshape(k // 512, 128, 2 * n)
    return np.ascontiguousarray(words), np.ascontiguousarray(byte.astype(np.uint8).reshape(k // 512, 16, n))


def unpack_weight(words, scales, fmt):
    g, _, n = scales.shape
    words = np.ascontiguousarray(words).reshape(g, 128, n, -1)
    if fmt == "e4m3":
        vals = words.view(ml_dtypes.float8_e4m3fn).astype(np.float64)
    else:
        nib = np.empty((g, 128, n, 4), np.uint8)
        nib[..., 0::2] = words & 0xF
        nib[..., 1::2] = words >> 4
        vals = E2M1[nib]
    vals = vals * np.repeat(np.exp2(scales.astype(np.float64) - 127.0), 8, axis=1)[..., None]
    return vals.transpose(0, 1, 3, 2).reshape(g * 512, n)


def gelu(v):
    return 0.5 * v * (1.0 + np.tanh(np.sqrt(2.0 / np.pi) * (v + 0.044715 * v**3)))


def striped8(idx):
    return np.concatenate([v.reshape(-1, 16).T for v in idx]).astype(np.uint16)


def unstriped8(offs):
    return np.stack([offs[16 * g:16 * g + 16].T.reshape(-1) for g in range(8)]).astype(np.int64)


def heads(h, wgt, idx8):
    r = np.arange(h.shape[0])
    return wgt[r // 4 % 128] * h[r[:, None], idx8[r % 512 // 64]]


K, H, N, T, S, T2, P = 1024, 1024, 384, 2048, 512, 1024, 512


def setup_inputs():
    n = np.random.standard_normal
    s = mx_kscale(K)[:, None]
    u = mx_kscale(H)[:, None]
    tab_words, tab_scales = pack_weight(n((K, T)) * s, "e4m3")
    w2_words, w2_scales = pack_weight(n((K, H)) / np.sqrt(K) / s * u.T, "e2m1")
    w5_words, w5_scales = pack_weight(n((H, N)) / np.sqrt(H) / u, "e4m3")
    links = np.stack([np.random.permutation(T2)[:P] for _ in range(8)])
    return {
        "tab_words": tab_words, "tab_scales": tab_scales,
        "offs": striped(np.random.permutation(T)[:S]),
        "w1": (n((K, H)) / np.sqrt(K) / s * u.T).astype(np.float32),
        "w2_words": w2_words, "w2_scales": w2_scales,
        "w3": (0.5 * n((K, H)) / np.sqrt(K) / s).astype(np.float32),
        "page0": (n((H, T2)) * u).astype(np.float32),
        "offs2": striped(np.random.permutation(T2)[:S]),
        "wgs": np.exp(0.3 * n((128, S))).astype(np.float32),
        "offs3": striped8(links),
        "wgt": np.repeat(np.random.uniform(0.5, 2.0, (8, P)), 16, axis=0).astype(np.float32),
        "w4": (n((H, N)) / np.sqrt(H) / u).astype(np.float32),
        "w5_words": w5_words, "w5_scales": w5_scales,
        "margin": n(N).astype(np.float32),
    }


def reference(tab_words, tab_scales, offs, w1, w2_words, w2_scales, w3, page0, offs2, wgs,
              offs3, wgt, w4, w5_words, w5_scales, margin):
    v = unpack_weight(tab_words, tab_scales, "e4m3")[:, unstriped(offs)]
    near = mxq(f64(w1), 0, "e4m3").T @ v
    reach = unpack_weight(w2_words, w2_scales, "e2m1").T @ v
    angle = mxq(f64(w3), 0, "e4m3").T @ v
    h = np.maximum(near, reach) * np.cos(angle)
    page = f64(page0).copy()
    page[:, unstriped(offs2)] = np.tile(f64(wgs), (H // 128, 1)) * h
    x = mxq(heads(page, f64(wgt), unstriped8(offs3)), 0, "e4m3")
    y1 = mxq(f64(w4), 0, "e4m3").T @ x
    y2 = unpack_weight(w5_words, w5_scales, "e4m3").T @ x
    return (y1 + f64(margin)[:, None]) * y2

@@ -1,0 +1,335 @@
+import math
+from contextlib import ExitStack
+
+import concourse.mybir as mybir
+from concourse.masks import make_identity
+
+K, H, N, T, S, T2, M = 1024, 1024, 384, 2048, 512, 1024, 512
+FLOPS = 2 * 3 * K * H * S + 2 * 2 * H * N * M
+
+F32 = mybir.dt.float32
+BF16 = mybir.dt.bfloat16
+I32 = mybir.dt.int32
+U32 = mybir.dt.uint32
+U16 = mybir.dt.uint16
+U8 = mybir.dt.uint8
+FP8X4 = mybir.dt.float8_e4m3fn_x4
+FP4X4 = mybir.dt.float4_e2m1fn_x4
+ALU = mybir.AluOpType
+ACT = mybir.ActivationFunctionType
+
+P = 128
+PACK = 4
+PASS = P * PACK
+PASSES = 2
+SLICES = PASSES * PACK
+N_TILES = N // P
+CHUNKS = 4
+CHUNK = M // CHUNKS
+REACH_BANK = (0, 3, 1, 0, 0, 1, 2, 3)
+ANGLE_BANK = (2, 3, 2, 1, 0, 1, 2, 3)
+
+
+def tile_list_proximity_limit_features_kernel(
+    tc, tab_words, tab_scales, offs, w1, w2_words, w2_scales, w3, page0, offs2, wgs,
+    offs3, wgt, w4, w5_words, w5_scales, margin, out,
+):
+    nc = tc.nc
+    with ExitStack() as ctx:
+        keep = ctx.enter_context(tc.tile_pool(name="keep", bufs=1))
+        ring = ctx.enter_context(tc.tile_pool(name="ring", bufs=4))
+        psum = ctx.enter_context(tc.psum_pool(name="psum", bufs=1))
+
+        def kept(shape, dtype, name):
+            return keep.tile(shape, dtype, name=name, align_bytes=64)
+
+        def load_scale_rows(queue, plane, rows):
+            for q in range(4):
+                queue.dma_start(
+                    out=plane[32 * q : 32 * q + 4, :, :].bitcast(I32),
+                    in_=rows[:, 4 * q : 4 * q + 4, :].rearrange("a r c -> r a c").bitcast(I32),
+                )
+
+        def clear(plane):
+            nc.vector.memset(plane[:].rearrange("p a c -> p (a c)").bitcast(I32), 0)
+
+        tab_plane = kept([P, PASSES, T], U8, "tab_plane")
+        w2_plane_raw = kept([P, PASSES, H], U8, "w2_plane_raw")
+        w5_plane = kept([P, PASSES, N], U8, "w5_plane")
+        nc.gpsimd.memset(tab_plane[:, 0, :].bitcast(I32), 0)
+        nc.vector.memset(tab_plane[:, 1, :].bitcast(I32), 0)
+        clear(w2_plane_raw)
+        clear(w5_plane)
+        ident = kept([P, P], F32, "ident")
+        make_identity(nc, ident[:])
+
+        def load_list(dram, name):
+            t = keep.tile([P, S // 16], U16, name=name)
+            nc.sync.dma_start(t[:], dram)
+            return t
+
+        def load_half(w, b, a, raw=None):
+            if raw is None:
+                raw = ring.tile([P, PACK, PASS], F32, name="raw", bufs=3)
+            nc.sync.dma_start(
+                out=raw[:],
+                in_=w[a * PASS : (a + 1) * PASS, b * PASS : (b + 1) * PASS].rearrange("(p j) c -> p j c", j=PACK),
+            )
+            return raw
+
+        page_rows = page0.rearrange("(b p i) t -> b i p t", b=PASSES, i=PACK)
+
+        def load_page(s):
+            t = kept([P, T2], F32, "page%d" % s)
+            nc.sync.dma_start(out=t[:], in_=page_rows[s // PACK, s % PACK])
+            return t
+
+        wgs_rows = wgs.rearrange("(q i) j -> q i j", i=PACK)
+
+        def load_wgs(first, count, name):
+            t = kept([P, count, S], F32, name)
+            for q in (0, 2, 1, 3):
+                nc.sync.dma_start(out=t[32 * q : 32 * q + 32, :, :], in_=wgs_rows[:, first : first + count, :])
+            return t
+
+        pick = load_list(offs, "pick")
+        w2_raw = kept([P, PASSES, H // 2], I32, "w2_raw")
+        nc.sync.dma_start(out=w2_raw[:], in_=w2_words.rearrange("a p c -> p a c").bitcast(I32))
+        tab = [kept([P, T], I32, "tab%d" % a) for a in range(PASSES)]
+        nc.sync.dma_start(out=tab[0][:], in_=tab_words[0].rearrange("p t i -> p (t i)").bitcast(I32))
+        load_scale_rows(nc.sync, tab_plane, tab_scales)
+        nc.sync.dma_start(out=tab[1][:], in_=tab_words[1].rearrange("p t i -> p (t i)").bitcast(I32))
+        load_scale_rows(nc.sync, w2_plane_raw, w2_scales)
+        first_raw = [kept([P, PACK, PASS], F32, "first_raw%d" % b) for b in range(PASSES)]
+        w3_raw = {(0, 0): load_half(w3, 0, 0, first_raw[0]), (0, 1): load_half(w3, 0, 1)}
+        w1_raw = {(0, a): load_half(w1, 0, a) for a in range(PASSES)}
+        place = load_list(offs2, "place")
+        wgs_first = load_wgs(0, 1, "wgs_first")
+        pages = [load_page(0)]
+        links = load_list(offs3, "links")
+        wgt_sb = kept([P, M], F32, "wgt_sb")
+        nc.sync.dma_start(out=wgt_sb[:], in_=wgt)
+        pages.append(load_page(1))
+        wgs_rest = load_wgs(1, PACK - 1, "wgs_rest")
+        wgs_of = [wgs_first[:, 0, :]] + [wgs_rest[:, i, :] for i in range(PACK - 1)]
+
+        w2_codes = kept([P, PASSES * H // 2], I32, "w2_codes")
+        nc.vector.tensor_copy(
+            out=w2_codes[:].bitcast(U16).rearrange("p (g t q) -> p g q t", t=PACK, q=P),
+            in_=w2_raw[:].rearrange("p a c -> p (a c)").bitcast(U16).rearrange("p (g q t) -> p g q t", t=PACK, q=P),
+        )
+        v_codes = kept([P, PASSES, S], U32, "v_codes")
+        v_plane = kept([P, PASSES, S], U8, "v_plane")
+        nc.vector.tensor_copy(out=v_codes[:, 0, :], in_=tab[0][:].bitcast(U32).indirect(pick[:]))
+        for a in range(PASSES):
+            nc.vector.tensor_copy(out=v_plane[:, a, :], in_=tab_plane[:, a, :].indirect(pick[:]))
+        nc.vector.tensor_copy(out=v_codes[:, 1, :], in_=tab[1][:].bitcast(U32).indirect(pick[:]))
+        w2_plane = kept([P, PASSES * H], U8, "w2_plane")
+        nc.vector.tensor_copy(
+            out=w2_plane[:].rearrange("p (g t q) -> p g q t", t=PACK, q=P),
+            in_=w2_plane_raw[:].rearrange("p a (b q t) -> p (a b) q t", t=PACK, q=P),
+        )
+
+        def quantise_half(raw, name, on_vector, stage):
+            dst = stage[:].rearrange("p (t q j) -> p q j t", t=PACK, j=PACK)
+            src = raw[:].rearrange("p j (q t) -> p q j t", t=PACK)
+            if on_vector:
+                nc.vector.tensor_copy(out=dst, in_=src)
+            else:
+                nc.scalar.copy(out=dst, in_=src)
+            codes = kept([P, PASS], U32, name + "_codes")
+            plane = kept([P, PASS], U8, name + "_plane")
+            nc.vector.quantize_mx(out=codes[:].bitcast(FP8X4), scales=plane[:], in_=stage[:])
+            return codes, plane
+
+        def stage_tile():
+            return ring.tile([P, PACK * PASS], BF16, name="stage", bufs=2, align_bytes=64)
+
+        w1_q, w3_q = {}, {}
+        w3_q[0, 0] = quantise_half(w3_raw[0, 0], "w3_00", False, stage_tile())
+        w3_q[0, 1] = quantise_half(w3_raw[0, 1], "w3_01", True, stage_tile())
+
+        picked = [kept([P, PACK, M], F32, "picked%d" % b) for b in range(PASSES)]
+        whole_first = kept([P, S], F32, "whole_first")
+        w4_stage = kept([P, PASSES * PACK * N], BF16, "w4_stage")
+        x0_stage = kept([P, PACK * M], BF16, "x0_stage")
+        w3_second_stage = kept([P, PASSES * PACK * PASS], BF16, "w3_second_stage")
+        w1_last_stage = kept([P, PACK * PASS], BF16, "w1_last_stage")
+
+        reach_sb, turns, cosine = {}, {}, {}
+        banks = [psum.tile([P, S], F32, name="bank%d" % n) for n in range(8)]
+
+        def reach_of(s):
+            b, i = divmod(s, PACK)
+            bank = banks[REACH_BANK[s]]
+            for a in range(PASSES):
+                c0 = a * H + s * P
+                nc.tensor.matmul_mx(
+                    out=bank[:],
+                    lhsT=w2_codes[:].bitcast(U8)[:, 2 * c0 : 2 * (c0 + P)].bitcast(FP4X4),
+                    lhsT_scale=w2_plane[:, c0 : c0 + P],
+                    rhs=v_codes[:, a, :].bitcast(FP8X4), rhs_scale=v_plane[:, a, :],
+                    start=(a == 0), stop=(a == PASSES - 1),
+                )
+            reach_sb[s] = whole_first[:] if s == 2 else first_raw[b][:, i, :]
+            nc.scalar.copy(out=reach_sb[s], in_=bank[:])
+
+        def cosine_of(s):
+            b, i = divmod(s, PACK)
+            angle = banks[ANGLE_BANK[s]]
+            for jb in range(S // P):
+                for a in ((0, 1), (1, 0))[b]:
+                    codes, plane = w3_q[b, a]
+                    nc.tensor.matmul_mx(
+                        out=angle[:, jb * P : (jb + 1) * P],
+                        lhsT=v_codes[:, a, jb * P : (jb + 1) * P].bitcast(FP8X4),
+                        lhsT_scale=v_plane[:, a, jb * P : (jb + 1) * P],
+                        rhs=codes[:, i * P : (i + 1) * P].bitcast(FP8X4), rhs_scale=plane[:, i * P : (i + 1) * P],
+                        start=(a == b), stop=(a != b),
+                    )
+            turns[s] = ring.tile([P, S], F32, name="turns")
+            nc.scalar.activation(out=turns[s][:], in_=angle[:], func=ACT.Abs, scale=1.0 / (2.0 * math.pi))
+            if s == 0:
+                count = first_raw[0][:, 1, :].bitcast(U32)
+            elif s == 3:
+                count = w3_second_stage[:, 1536:2560].bitcast(U32)
+            elif s == 5:
+                count = w4_stage[:, 1024:2048].bitcast(U32)
+            elif s == 7:
+                count = x0_stage[:, 0:1024].bitcast(U32)
+            else:
+                count = ring.tile([P, S], U32, name="count", bufs=2)[:]
+            nc.scalar.activation(out=count, in_=turns[s][:], func=ACT.Copy, bias=0.25)
+            whole = whole_first[:] if s == 0 else picked[(s - 1) // PACK][:, (s - 1) % PACK, :]
+            nc.scalar.activation(out=whole, in_=count, func=ACT.Copy, scale=-1.0, bias=0.25)
+            frac = angle
+            for term, part in enumerate((turns[s][:], whole)):
+                for jb in range(S // P):
+                    cols = slice(jb * P, (jb + 1) * P)
+                    nc.tensor.matmul(
+                        frac[:, cols], lhsT=part[:, cols], rhs=ident[:], is_transpose=True,
+                        start=(term == 0 and jb == 0), stop=(term == 1 and jb == S // P - 1),
+                    )
+            cosine[s] = ring.tile([P, S], F32, name="cosine")
+            nc.scalar.activation(out=cosine[s][:], in_=frac[:], func=ACT.Sin, scale=2.0 * math.pi)
+
+        def gather(s, c0, c1):
+            b, i = divmod(s, PACK)
+            nc.vector.tensor_tensor(
+                out=picked[b][:, i, c0:c1], in0=pages[s][:].indirect(links[:, c0 // 16 : c1 // 16]),
+                in1=wgt_sb[:, c0:c1], op=ALU.mult,
+            )
+
+        def interleave(stage, planes, on_vector=False):
+            copy = nc.vector.tensor_copy if on_vector else nc.scalar.copy
+            copy(
+                out=stage.rearrange("p (c i j) -> p c j i", i=4, j=PACK),
+                in_=planes.rearrange("p j (c i) -> p c j i", i=4),
+            )
+
+        reach_of(0)
+        cosine_of(0)
+        for a in range(PASSES):
+            w1_q[0, a] = quantise_half(w1_raw[0, a], "w1_0%d" % a, True, stage_tile())
+
+        w3_raw[1, 0] = load_half(w3, 1, 0, first_raw[1])
+        w3_raw[1, 1] = load_half(w3, 1, 1)
+        pages.append(load_page(2))
+        for a in range(PASSES):
+            w1_raw[1, a] = load_half(w1, 1, a)
+        for s in range(3, SLICES):
+            pages.append(load_page(s))
+        w4_raw = []
+        for a in range(PASSES):
+            raw = ring.tile([P, PACK, N], F32, name="raw", bufs=3)
+            nc.sync.dma_start(out=raw[:], in_=w4[a * PASS : (a + 1) * PASS, :].rearrange("(p j) c -> p j c", j=PACK))
+            w4_raw.append(raw)
+        w5_codes = kept([P, PASSES, N], I32, "w5_codes")
+        nc.sync.dma_start(out=w5_codes[:], in_=w5_words.rearrange("a p c i -> p a (c i)").bitcast(I32))
+        load_scale_rows(nc.sync, w5_plane, w5_scales)
+        margin_sb = kept([P, N_TILES], F32, "margin_sb")
+        with nc.allow_non_contiguous_dma(reason="one margin value a partition"):
+            nc.sync.dma_start(out=margin_sb[:], in_=margin.rearrange("(n p) -> p n", p=P))
+
+        w4_codes = kept([P, PASSES, N], U32, "w4_codes")
+        w4_plane = kept([P, PASSES, N], U8, "w4_plane")
+        x0_codes = kept([P, M], U32, "x0_codes")
+        x0_plane = kept([P, M], U8, "x0_plane")
+
+        for s in range(SLICES):
+            b, i = divmod(s, PACK)
+            near = banks[4 + i]
+            for a in ((0, 1), (1, 0))[b]:
+                codes, plane = w1_q[b, a]
+                nc.tensor.matmul_mx(
+                    out=near[:],
+                    lhsT=codes[:, i * P : (i + 1) * P].bitcast(FP8X4), lhsT_scale=plane[:, i * P : (i + 1) * P],
+                    rhs=v_codes[:, a, :].bitcast(FP8X4), rhs_scale=v_plane[:, a, :],
+                    start=(a == b), stop=(a != b),
+                )
+            nc.vector.tensor_tensor(out=turns[s][:], in0=near[:], in1=reach_sb[s], op=ALU.max)
+            if s > 0:
+                gather(s - 1, 0, M)
+            if s == PACK - 1:
+                w3_q[1, 0] = quantise_half(w3_raw[1, 0], "w3_10", False, w3_second_stage[:, 0 : PACK * PASS])
+                w3_q[1, 1] = quantise_half(w3_raw[1, 1], "w3_11", False, w3_second_stage[:, PACK * PASS :])
+                w1_q[1, 0] = quantise_half(w1_raw[1, 0], "w1_10", False, stage_tile())
+                w1_q[1, 1] = quantise_half(w1_raw[1, 1], "w1_11", False, w1_last_stage)
+                weighted = w1_last_stage[:, 0 : 2 * S].bitcast(F32)
+            else:
+                weighted = cosine[s][:]
+            nc.vector.tensor_tensor(out=weighted, in0=cosine[s][:], in1=wgs_of[i], op=ALU.mult)
+            nc.vector.tensor_tensor(out=pages[s][:].indirect(place[:]), in0=turns[s][:], in1=weighted, op=ALU.mult)
+            if s + 1 < SLICES:
+                reach_of(s + 1)
+                cosine_of(s + 1)
+            if s == 5:
+                for a in range(PASSES):
+                    stage = w4_stage[:, a * PACK * N : (a + 1) * PACK * N]
+                    interleave(stage, w4_raw[a][:])
+                    nc.vector.quantize_mx(out=w4_codes[:, a, :].bitcast(FP8X4), scales=w4_plane[:, a, :], in_=stage)
+            if s == 6:
+                interleave(x0_stage[:], picked[0][:])
+                nc.vector.quantize_mx(out=x0_codes[:].bitcast(FP8X4), scales=x0_plane[:], in_=x0_stage[:])
+
+
+        weights = ((w4_codes, w4_plane), (w5_codes, w5_plane))
+        y_banks = [banks[2 * c : 2 * c + 2] for c in range(CHUNKS)]
+
+        def second_stage(c, b, x_codes, x_plane):
+            for y in (1, 0):
+                codes, plane = weights[y]
+                for n in range(N_TILES):
+                    nc.tensor.matmul_mx(
+                        out=y_banks[c][y][:, n * CHUNK : (n + 1) * CHUNK],
+                        lhsT=codes[:, b, n * P : (n + 1) * P].bitcast(FP8X4), lhsT_scale=plane[:, b, n * P : (n + 1) * P],
+                        rhs=x_codes.bitcast(FP8X4), rhs_scale=x_plane,
+                        start=(b == 0 and n == 0), stop=(b == PASSES - 1 and n == N_TILES - 1),
+                    )
+
+        for c in range(CHUNKS):
+            cols = slice(c * CHUNK, (c + 1) * CHUNK)
+            second_stage(c, 0, x0_codes[:, cols], x0_plane[:, cols])
+        for c in range(CHUNKS):
+            gather(SLICES - 1, c * CHUNK, (c + 1) * CHUNK)
+        out_rows = out.rearrange("(n p) m -> p n m", p=P)
+        stages = [kept([P, PACK * CHUNK], BF16, "x1_stage%d" % c) for c in range(CHUNKS)]
+        for c in range(CHUNKS):
+            interleave(stages[c][:], picked[1][:, :, c * CHUNK : (c + 1) * CHUNK], c >= CHUNKS // 2)
+        for c in range(CHUNKS):
+            stage = stages[c]
+            x_codes = kept([P, CHUNK], U32, "x1_codes%d" % c)
+            x_plane = kept([P, CHUNK], U8, "x1_plane%d" % c)
+            nc.vector.quantize_mx(out=x_codes[:].bitcast(FP8X4), scales=x_plane[:], in_=stage[:])
+            second_stage(c, 1, x_codes[:], x_plane[:])
+        for c in range(CHUNKS):
+            cols = slice(c * CHUNK, (c + 1) * CHUNK)
+            y2 = ring.tile([P, N_TILES * CHUNK], F32, name="y2", bufs=2)
+            nc.scalar.copy(out=y2[:], in_=y_banks[c][1][:, 0 : N_TILES * CHUNK])
+            res = ring.tile([P, N_TILES, CHUNK], F32, name="res")
+            for n in range(N_TILES):
+                nc.vector.scalar_tensor_tensor(
+                    out=res[:, n, :], in0=y_banks[c][0][:, n * CHUNK : (n + 1) * CHUNK], scalar=margin_sb[:, n : n + 1],
+                    in1=y2[:, n * CHUNK : (n + 1) * CHUNK], op0=ALU.add, op1=ALU.mult,
+                )
+            nc.sync.dma_start(out=out_rows[:, :, cols], in_=res[:])

@@ -26,8 +26,8 @@ SLICES = PASSES * PACK
 N_TILES = N // P
 CHUNKS = 4
 CHUNK = M // CHUNKS
-REACH_BANK = (0, 3, 1, 0, 0, 1, 2, 3)
-ANGLE_BANK = (2, 3, 2, 1, 0, 1, 2, 3)
+REACH_BANK = (0, 3, 1, 7, 0, 2, 3, 1)
+ANGLE_BANK = (2, 0, 2, 3, 1, 0, 2, 3)
 
 
 def tile_list_proximity_limit_features_kernel(
@@ -44,7 +44,7 @@ def tile_list_proximity_limit_features_kernel(
             return keep.tile(shape, dtype, name=name, align_bytes=64)
 
         def load_scale_rows(queue, plane, rows):
-            for q in range(4):
+            for q in (0, 2, 1, 3):
                 queue.dma_start(
                     out=plane[32 * q : 32 * q + 4, :, :].bitcast(I32),
                     in_=rows[:, 4 * q : 4 * q + 4, :].rearrange("a r c -> r a c").bitcast(I32),
@@ -115,8 +115,8 @@ def tile_list_proximity_limit_features_kernel(
 
         w2_codes = kept([P, PASSES * H // 2], I32, "w2_codes")
         nc.vector.tensor_copy(
-            out=w2_codes[:].bitcast(U16).rearrange("p (g t q) -> p g q t", t=PACK, q=P),
-            in_=w2_raw[:].rearrange("p a c -> p (a c)").bitcast(U16).rearrange("p (g q t) -> p g q t", t=PACK, q=P),
+            out=w2_codes[:].bitcast(U16).rearrange("p (g t q) -> p g t q", t=PACK, q=P),
+            in_=w2_raw[:].rearrange("p a c -> p (a c)").bitcast(U16).rearrange("p (g q t) -> p g t q", t=PACK, q=P),
         )
         v_codes = kept([P, PASSES, S], U32, "v_codes")
         v_plane = kept([P, PASSES, S], U8, "v_plane")
@@ -126,31 +126,35 @@ def tile_list_proximity_limit_features_kernel(
         nc.vector.tensor_copy(out=v_codes[:, 1, :], in_=tab[1][:].bitcast(U32).indirect(pick[:]))
         w2_plane = kept([P, PASSES * H], U8, "w2_plane")
         nc.vector.tensor_copy(
-            out=w2_plane[:].rearrange("p (g t q) -> p g q t", t=PACK, q=P),
-            in_=w2_plane_raw[:].rearrange("p a (b q t) -> p (a b) q t", t=PACK, q=P),
+            out=w2_plane[:].rearrange("p (g t q) -> p g t q", t=PACK, q=P),
+            in_=w2_plane_raw[:].rearrange("p a (b q t) -> p (a b) t q", t=PACK, q=P),
         )
 
-        def quantise_half(raw, name, on_vector, stage):
-            dst = stage[:].rearrange("p (t q j) -> p q j t", t=PACK, j=PACK)
-            src = raw[:].rearrange("p j (q t) -> p q j t", t=PACK)
-            if on_vector:
-                nc.vector.tensor_copy(out=dst, in_=src)
-            else:
-                nc.scalar.copy(out=dst, in_=src)
-            codes = kept([P, PASS], U32, name + "_codes")
-            plane = kept([P, PASS], U8, name + "_plane")
-            nc.vector.quantize_mx(out=codes[:].bitcast(FP8X4), scales=plane[:], in_=stage[:])
-            return codes, plane
+        def operand(name):
+            return kept([P, PASS], U32, name + "_codes"), kept([P, PASS], U8, name + "_plane")
+
+        def quantise(dest, raw, stage, on_vector, first=0, last=PACK):
+            copy = nc.vector.tensor_copy if on_vector else nc.scalar.copy
+            part = stage[:, 0 : (last - first) * PASS] if on_vector else stage[:, first * PASS : last * PASS]
+            copy(
+                out=part.rearrange("p (t q j) -> p q j t", q=P, j=PACK),
+                in_=raw[:].rearrange("p j (q t) -> p q j t", t=PACK)[:, :, :, first:last],
+            )
+            codes, plane = dest
+            cols = slice(first * P, last * P)
+            nc.vector.quantize_mx(out=codes[:, cols].bitcast(FP8X4), scales=plane[:, cols], in_=part)
 
         def stage_tile():
-            return ring.tile([P, PACK * PASS], BF16, name="stage", bufs=2, align_bytes=64)
+            return ring.tile([P, PACK * PASS], BF16, name="stage", bufs=3, align_bytes=64)
 
-        w1_q, w3_q = {}, {}
-        w3_q[0, 0] = quantise_half(w3_raw[0, 0], "w3_00", False, stage_tile())
-        w3_q[0, 1] = quantise_half(w3_raw[0, 1], "w3_01", True, stage_tile())
+        w1_q = {(b, a): operand("w1_%d%d" % (b, a)) for b in range(PASSES) for a in range(PASSES)}
+        w3_q = {(b, a): operand("w3_%d%d" % (b, a)) for b in range(PASSES) for a in range(PASSES)}
+        w3_stage = [stage_tile() for a in range(PASSES)]
+        for a in range(PASSES):
+            quantise(w3_q[0, a], w3_raw[0, a], w3_stage[a], a == 1, 0, 1)
+        quantise(w3_q[0, 0], w3_raw[0, 0], w3_stage[0], False, 1, PACK)
 
         picked = [kept([P, PACK, M], F32, "picked%d" % b) for b in range(PASSES)]
-        whole_first = kept([P, S], F32, "whole_first")
         w4_stage = kept([P, PASSES * PACK * N], BF16, "w4_stage")
         x0_stage = kept([P, PACK * M], BF16, "x0_stage")
         w3_second_stage = kept([P, PASSES * PACK * PASS], BF16, "w3_second_stage")
@@ -171,7 +175,7 @@ def tile_list_proximity_limit_features_kernel(
                     rhs=v_codes[:, a, :].bitcast(FP8X4), rhs_scale=v_plane[:, a, :],
                     start=(a == 0), stop=(a == PASSES - 1),
                 )
-            reach_sb[s] = whole_first[:] if s == 2 else first_raw[b][:, i, :]
+            reach_sb[s] = first_raw[b][:, (1, 0, 2, 3)[s] if b == 0 else i, :]
             nc.scalar.copy(out=reach_sb[s], in_=bank[:])
 
         def cosine_of(s):
@@ -187,10 +191,13 @@ def tile_list_proximity_limit_features_kernel(
                         rhs=codes[:, i * P : (i + 1) * P].bitcast(FP8X4), rhs_scale=plane[:, i * P : (i + 1) * P],
                         start=(a == b), stop=(a != b),
                     )
-            turns[s] = ring.tile([P, S], F32, name="turns")
+            if s == SLICES - 1:
+                turns[s] = kept([P, S], F32, "last")
+            else:
+                turns[s] = ring.tile([P, S], F32, name="turns")
             nc.scalar.activation(out=turns[s][:], in_=angle[:], func=ACT.Abs, scale=1.0 / (2.0 * math.pi))
-            if s == 0:
-                count = first_raw[0][:, 1, :].bitcast(U32)
+            if s < 3:
+                count = first_raw[0][:, s + 1, :].bitcast(U32)
             elif s == 3:
                 count = w3_second_stage[:, 1536:2560].bitcast(U32)
             elif s == 5:
@@ -198,9 +205,9 @@ def tile_list_proximity_limit_features_kernel(
             elif s == 7:
                 count = x0_stage[:, 0:1024].bitcast(U32)
             else:
-                count = ring.tile([P, S], U32, name="count", bufs=2)[:]
+                count = ring.tile([P, S], U32, name="count", bufs=1)[:]
             nc.scalar.activation(out=count, in_=turns[s][:], func=ACT.Copy, bias=0.25)
-            whole = whole_first[:] if s == 0 else picked[(s - 1) // PACK][:, (s - 1) % PACK, :]
+            whole = first_raw[0][:, 0, :] if s == 0 else picked[(s - 1) // PACK][:, (s - 1) % PACK, :]
             nc.scalar.activation(out=whole, in_=count, func=ACT.Copy, scale=-1.0, bias=0.25)
             frac = angle
             for term, part in enumerate((turns[s][:], whole)):
@@ -227,10 +234,12 @@ def tile_list_proximity_limit_features_kernel(
                 in_=planes.rearrange("p j (c i) -> p c j i", i=4),
             )
 
-        reach_of(0)
         cosine_of(0)
-        for a in range(PASSES):
-            w1_q[0, a] = quantise_half(w1_raw[0, a], "w1_0%d" % a, True, stage_tile())
+        reach_of(0)
+        quantise(w3_q[0, 1], w3_raw[0, 1], w3_stage[1], True, 1, PACK)
+        quantise(w1_q[0, 0], w1_raw[0, 0], stage_tile(), True)
+        w1_stage = stage_tile()
+        quantise(w1_q[0, 1], w1_raw[0, 1], w1_stage, True, 0, 1)
 
         w3_raw[1, 0] = load_half(w3, 1, 0, first_raw[1])
         w3_raw[1, 1] = load_half(w3, 1, 1)
@@ -253,34 +262,40 @@ def tile_list_proximity_limit_features_kernel(
 
         w4_codes = kept([P, PASSES, N], U32, "w4_codes")
         w4_plane = kept([P, PASSES, N], U8, "w4_plane")
-        x0_codes = kept([P, M], U32, "x0_codes")
-        x0_plane = kept([P, M], U8, "x0_plane")
+        x0_codes = [kept([P, M // 2], U32, "x0_codes")]
+        x0_plane = [kept([P, M // 2], U8, "x0_plane%d" % h) for h in range(2)]
 
         for s in range(SLICES):
             b, i = divmod(s, PACK)
             near = banks[4 + i]
-            for a in ((0, 1), (1, 0))[b]:
+            order = (0, 1) if s == 0 else (1, 0)
+            for a in order:
                 codes, plane = w1_q[b, a]
                 nc.tensor.matmul_mx(
                     out=near[:],
                     lhsT=codes[:, i * P : (i + 1) * P].bitcast(FP8X4), lhsT_scale=plane[:, i * P : (i + 1) * P],
                     rhs=v_codes[:, a, :].bitcast(FP8X4), rhs_scale=v_plane[:, a, :],
-                    start=(a == b), stop=(a != b),
+                    start=(a == order[0]), stop=(a == order[1]),
                 )
             nc.vector.tensor_tensor(out=turns[s][:], in0=near[:], in1=reach_sb[s], op=ALU.max)
             if s > 0:
                 gather(s - 1, 0, M)
             if s == PACK - 1:
-                w3_q[1, 0] = quantise_half(w3_raw[1, 0], "w3_10", False, w3_second_stage[:, 0 : PACK * PASS])
-                w3_q[1, 1] = quantise_half(w3_raw[1, 1], "w3_11", False, w3_second_stage[:, PACK * PASS :])
-                w1_q[1, 0] = quantise_half(w1_raw[1, 0], "w1_10", False, stage_tile())
-                w1_q[1, 1] = quantise_half(w1_raw[1, 1], "w1_11", False, w1_last_stage)
+                for a in range(PASSES):
+                    quantise(w3_q[1, a], w3_raw[1, a], w3_second_stage[:, a * PACK * PASS : (a + 1) * PACK * PASS], False)
+                quantise(w1_q[1, 0], w1_raw[1, 0], stage_tile(), False)
+                quantise(w1_q[1, 1], w1_raw[1, 1], w1_last_stage, False)
                 weighted = w1_last_stage[:, 0 : 2 * S].bitcast(F32)
             else:
                 weighted = cosine[s][:]
             nc.vector.tensor_tensor(out=weighted, in0=cosine[s][:], in1=wgs_of[i], op=ALU.mult)
             nc.vector.tensor_tensor(out=pages[s][:].indirect(place[:]), in0=turns[s][:], in1=weighted, op=ALU.mult)
-            if s + 1 < SLICES:
+            if s == 0:
+                quantise(w1_q[0, 1], w1_raw[0, 1], w1_stage, True, 1, PACK)
+            if s + 1 == PACK:
+                cosine_of(s + 1)
+                reach_of(s + 1)
+            elif s + 1 < SLICES:
                 reach_of(s + 1)
                 cosine_of(s + 1)
             if s == 5:
@@ -290,7 +305,7 @@ def tile_list_proximity_limit_features_kernel(
                     nc.vector.quantize_mx(out=w4_codes[:, a, :].bitcast(FP8X4), scales=w4_plane[:, a, :], in_=stage)
             if s == 6:
                 interleave(x0_stage[:], picked[0][:])
-                nc.vector.quantize_mx(out=x0_codes[:].bitcast(FP8X4), scales=x0_plane[:], in_=x0_stage[:])
+                nc.vector.quantize_mx(out=x0_codes[0][:].bitcast(FP8X4), scales=x0_plane[0][:], in_=x0_stage[:, 0 : 2 * M])
 
 
         weights = ((w4_codes, w4_plane), (w5_codes, w5_plane))
@@ -307,24 +322,23 @@ def tile_list_proximity_limit_features_kernel(
                         start=(b == 0 and n == 0), stop=(b == PASSES - 1 and n == N_TILES - 1),
                     )
 
+        x0_codes.append(kept([P, M // 2], U32, "last"))
+        nc.vector.quantize_mx(out=x0_codes[1][:].bitcast(FP8X4), scales=x0_plane[1][:], in_=x0_stage[:, 2 * M :])
         for c in range(CHUNKS):
-            cols = slice(c * CHUNK, (c + 1) * CHUNK)
-            second_stage(c, 0, x0_codes[:, cols], x0_plane[:, cols])
+            cols = slice(c % 2 * CHUNK, (c % 2 + 1) * CHUNK)
+            second_stage(c, 0, x0_codes[c // 2][:, cols], x0_plane[c // 2][:, cols])
+        out_rows = out.rearrange("(n p) m -> p n m", p=P)
         for c in range(CHUNKS):
             gather(SLICES - 1, c * CHUNK, (c + 1) * CHUNK)
-        out_rows = out.rearrange("(n p) m -> p n m", p=P)
-        stages = [kept([P, PACK * CHUNK], BF16, "x1_stage%d" % c) for c in range(CHUNKS)]
-        for c in range(CHUNKS):
-            interleave(stages[c][:], picked[1][:, :, c * CHUNK : (c + 1) * CHUNK], c >= CHUNKS // 2)
-        for c in range(CHUNKS):
-            stage = stages[c]
+            stage = kept([P, PACK * CHUNK], BF16, "x1_stage%d" % c)
+            interleave(stage[:], picked[1][:, :, c * CHUNK : (c + 1) * CHUNK], c == 0)
             x_codes = kept([P, CHUNK], U32, "x1_codes%d" % c)
             x_plane = kept([P, CHUNK], U8, "x1_plane%d" % c)
             nc.vector.quantize_mx(out=x_codes[:].bitcast(FP8X4), scales=x_plane[:], in_=stage[:])
             second_stage(c, 1, x_codes[:], x_plane[:])
         for c in range(CHUNKS):
             cols = slice(c * CHUNK, (c + 1) * CHUNK)
-            y2 = ring.tile([P, N_TILES * CHUNK], F32, name="y2", bufs=2)
+            y2 = ring.tile([P, N_TILES * CHUNK], F32, name="y2")
             nc.scalar.copy(out=y2[:], in_=y_banks[c][1][:, 0 : N_TILES * CHUNK])
             res = ring.tile([P, N_TILES, CHUNK], F32, name="res")
             for n in range(N_TILES):

@@ -26,8 +26,9 @@ SLICES = PASSES * PACK
 N_TILES = N // P
 CHUNKS = 4
 CHUNK = M // CHUNKS
-REACH_BANK = (0, 3, 1, 7, 0, 2, 3, 1)
-ANGLE_BANK = (2, 0, 2, 3, 1, 0, 2, 3)
+REACH_BANK = (0, 3, 1, 7, 3, 1, 7, 6)
+ANGLE_BANK = (2, 3, 1, 7, 6, 3, 1, 7)
+NEAR_BANK = (4, 2, 0, 5)
 
 
 def tile_list_proximity_limit_features_kernel(
@@ -62,6 +63,8 @@ def tile_list_proximity_limit_features_kernel(
         clear(w5_plane)
         ident = kept([P, P], F32, "ident")
         make_identity(nc, ident[:])
+        warm = kept([P, 1], F32, "warm")
+        nc.scalar.activation(out=warm[:], in_=ident[:, 0:1], func=ACT.Sin)
 
         def load_list(dram, name):
             t = keep.tile([P, S // 16], U16, name=name)
@@ -80,7 +83,10 @@ def tile_list_proximity_limit_features_kernel(
         page_rows = page0.rearrange("(b p i) t -> b i p t", b=PASSES, i=PACK)
 
         def load_page(s):
-            t = kept([P, T2], F32, "page%d" % s)
+            if s == SLICES - 1:
+                t = ring.tile([P, T2], F32, name="raw", bufs=3)
+            else:
+                t = kept([P, T2], F32, {4: "w2_raw", 5: "tab0", 6: "tab1"}.get(s, "page%d" % s))
             nc.sync.dma_start(out=t[:], in_=page_rows[s // PACK, s % PACK])
             return t
 
@@ -104,8 +110,8 @@ def tile_list_proximity_limit_features_kernel(
         w3_raw = {(0, 0): load_half(w3, 0, 0, first_raw[0]), (0, 1): load_half(w3, 0, 1)}
         w1_raw = {(0, a): load_half(w1, 0, a) for a in range(PASSES)}
         place = load_list(offs2, "place")
-        wgs_first = load_wgs(0, 1, "wgs_first")
         pages = [load_page(0)]
+        wgs_first = load_wgs(0, 1, "wgs_first")
         links = load_list(offs3, "links")
         wgt_sb = kept([P, M], F32, "wgt_sb")
         nc.sync.dma_start(out=wgt_sb[:], in_=wgt)
@@ -133,9 +139,8 @@ def tile_list_proximity_limit_features_kernel(
         def operand(name):
             return kept([P, PASS], U32, name + "_codes"), kept([P, PASS], U8, name + "_plane")
 
-        def quantise(dest, raw, stage, on_vector, first=0, last=PACK):
+        def quantise(dest, raw, part, on_vector, first=0, last=PACK):
             copy = nc.vector.tensor_copy if on_vector else nc.scalar.copy
-            part = stage[:, 0 : (last - first) * PASS] if on_vector else stage[:, first * PASS : last * PASS]
             copy(
                 out=part.rearrange("p (t q j) -> p q j t", q=P, j=PACK),
                 in_=raw[:].rearrange("p j (q t) -> p q j t", t=PACK)[:, :, :, first:last],
@@ -145,20 +150,20 @@ def tile_list_proximity_limit_features_kernel(
             nc.vector.quantize_mx(out=codes[:, cols].bitcast(FP8X4), scales=plane[:, cols], in_=part)
 
         def stage_tile():
-            return ring.tile([P, PACK * PASS], BF16, name="stage", bufs=3, align_bytes=64)
+            return ring.tile([P, PACK * PASS], BF16, name="stage", bufs=2, align_bytes=64)
 
         w1_q = {(b, a): operand("w1_%d%d" % (b, a)) for b in range(PASSES) for a in range(PASSES)}
         w3_q = {(b, a): operand("w3_%d%d" % (b, a)) for b in range(PASSES) for a in range(PASSES)}
-        w3_stage = [stage_tile() for a in range(PASSES)]
-        for a in range(PASSES):
-            quantise(w3_q[0, a], w3_raw[0, a], w3_stage[a], a == 1, 0, 1)
-        quantise(w3_q[0, 0], w3_raw[0, 0], w3_stage[0], False, 1, PACK)
+        quantise(w3_q[0, 0], w3_raw[0, 0], stage_tile()[:], True)
+        w3_stage = stage_tile()
+        quantise(w3_q[0, 1], w3_raw[0, 1], w3_stage[:, 0:PASS], True, 0, 1)
+        quantise(w3_q[0, 1], w3_raw[0, 1], w3_stage[:, PASS:], False, 1, PACK)
 
         picked = [kept([P, PACK, M], F32, "picked%d" % b) for b in range(PASSES)]
         w4_stage = kept([P, PASSES * PACK * N], BF16, "w4_stage")
+        w1_first_stage = kept([P, 5 * S], BF16, "w1_first_stage")
         x0_stage = kept([P, PACK * M], BF16, "x0_stage")
-        w3_second_stage = kept([P, PASSES * PACK * PASS], BF16, "w3_second_stage")
-        w1_last_stage = kept([P, PACK * PASS], BF16, "w1_last_stage")
+        second_stage_in = kept([P, 2 * PASSES, PACK * PASS], BF16, "second_half_stage")
 
         reach_sb, turns, cosine = {}, {}, {}
         banks = [psum.tile([P, S], F32, name="bank%d" % n) for n in range(8)]
@@ -175,7 +180,10 @@ def tile_list_proximity_limit_features_kernel(
                     rhs=v_codes[:, a, :].bitcast(FP8X4), rhs_scale=v_plane[:, a, :],
                     start=(a == 0), stop=(a == PASSES - 1),
                 )
-            reach_sb[s] = first_raw[b][:, (1, 0, 2, 3)[s] if b == 0 else i, :]
+            if s in (1, 2):
+                reach_sb[s] = w1_first_stage[:, (s - 1) * 3 * S : (s - 1) * 3 * S + 2 * S].bitcast(F32)
+            else:
+                reach_sb[s] = first_raw[b][:, (1, 0, 0, 2)[s] if b == 0 else i, :]
             nc.scalar.copy(out=reach_sb[s], in_=bank[:])
 
         def cosine_of(s):
@@ -199,16 +207,20 @@ def tile_list_proximity_limit_features_kernel(
             if s < 3:
                 count = first_raw[0][:, s + 1, :].bitcast(U32)
             elif s == 3:
-                count = w3_second_stage[:, 1536:2560].bitcast(U32)
+                count = second_stage_in[:, :, 0 : 2 * P].bitcast(U32)
+            elif s == 4:
+                count = first_raw[1][:].rearrange("p i c -> p (i c)")[:, 768:1280].bitcast(U32)
             elif s == 5:
                 count = w4_stage[:, 1024:2048].bitcast(U32)
             elif s == 7:
                 count = x0_stage[:, 0:1024].bitcast(U32)
             else:
-                count = ring.tile([P, S], U32, name="count", bufs=1)[:]
-            nc.scalar.activation(out=count, in_=turns[s][:], func=ACT.Copy, bias=0.25)
+                count = first_raw[0][:, PACK - 1, :].bitcast(U32)
+            runs = PACK if s == 3 else 1
+            count = count if s == 3 else count.rearrange("p (r c) -> p r c", r=runs)
+            nc.scalar.activation(out=count, in_=turns[s][:].rearrange("p (r c) -> p r c", r=runs), func=ACT.Copy, bias=0.25)
             whole = first_raw[0][:, 0, :] if s == 0 else picked[(s - 1) // PACK][:, (s - 1) % PACK, :]
-            nc.scalar.activation(out=whole, in_=count, func=ACT.Copy, scale=-1.0, bias=0.25)
+            nc.scalar.activation(out=whole.rearrange("p (r c) -> p r c", r=runs), in_=count, func=ACT.Copy, scale=-1.0, bias=0.25)
             frac = angle
             for term, part in enumerate((turns[s][:], whole)):
                 for jb in range(S // P):
@@ -236,16 +248,14 @@ def tile_list_proximity_limit_features_kernel(
 
         cosine_of(0)
         reach_of(0)
-        quantise(w3_q[0, 1], w3_raw[0, 1], w3_stage[1], True, 1, PACK)
-        quantise(w1_q[0, 0], w1_raw[0, 0], stage_tile(), True)
-        w1_stage = stage_tile()
-        quantise(w1_q[0, 1], w1_raw[0, 1], w1_stage, True, 0, 1)
+        quantise(w1_q[0, 0], w1_raw[0, 0], stage_tile()[:], True)
+        quantise(w1_q[0, 1], w1_raw[0, 1], w1_first_stage[:, 768:1280], True, 0, 1)
 
-        w3_raw[1, 0] = load_half(w3, 1, 0, first_raw[1])
-        w3_raw[1, 1] = load_half(w3, 1, 1)
-        pages.append(load_page(2))
         for a in range(PASSES):
-            w1_raw[1, a] = load_half(w1, 1, a)
+            w1_raw[1, a] = load_half(w1, 1, a, kept([P, PACK, PASS], F32, "w1_raw%d" % a))
+        pages.append(load_page(2))
+        w3_raw[1, 0] = load_half(w3, 1, 0, kept([P, PACK, PASS], F32, "w3_raw"))
+        w3_raw[1, 1] = load_half(w3, 1, 1, first_raw[1])
         for s in range(3, SLICES):
             pages.append(load_page(s))
         w4_raw = []
@@ -267,7 +277,7 @@ def tile_list_proximity_limit_features_kernel(
 
         for s in range(SLICES):
             b, i = divmod(s, PACK)
-            near = banks[4 + i]
+            near = banks[NEAR_BANK[i]]
             order = (0, 1) if s == 0 else (1, 0)
             for a in order:
                 codes, plane = w1_q[b, a]
@@ -277,21 +287,28 @@ def tile_list_proximity_limit_features_kernel(
                     rhs=v_codes[:, a, :].bitcast(FP8X4), rhs_scale=v_plane[:, a, :],
                     start=(a == order[0]), stop=(a == order[1]),
                 )
-            nc.vector.tensor_tensor(out=turns[s][:], in0=near[:], in1=reach_sb[s], op=ALU.max)
+            larger = {1: reach_sb[0], 2: turns[0][:]}.get(s, turns[s][:])
+            nc.vector.tensor_tensor(out=larger, in0=near[:], in1=reach_sb[s], op=ALU.max)
             if s > 0:
                 gather(s - 1, 0, M)
             if s == PACK - 1:
                 for a in range(PASSES):
-                    quantise(w3_q[1, a], w3_raw[1, a], w3_second_stage[:, a * PACK * PASS : (a + 1) * PACK * PASS], False)
-                quantise(w1_q[1, 0], w1_raw[1, 0], stage_tile(), False)
-                quantise(w1_q[1, 1], w1_raw[1, 1], w1_last_stage, False)
-                weighted = w1_last_stage[:, 0 : 2 * S].bitcast(F32)
+                    quantise(w1_q[1, a], w1_raw[1, a], second_stage_in[:, a, :], False)
+                quantise(w3_q[1, 0], w3_raw[1, 0], second_stage_in[:, 2, 0 : 2 * PASS], False, 0, 2)
+                quantise(w3_q[1, 1], w3_raw[1, 1], second_stage_in[:, 3, PASS : 3 * PASS], False, 0, 2)
+                quantise(w3_q[1, 1], w3_raw[1, 1], second_stage_in[:, 2, 2 * PASS :], False, 2, PACK)
+                quantise(w3_q[1, 0], w3_raw[1, 0], second_stage_in[:, 3, 2 * PASS :], False, 2, PACK)
+                weighted = second_stage_in[:, 3, 0 : 2 * S].bitcast(F32)
+            elif s == 0:
+                weighted = reach_sb[s]
+            elif s == SLICES - 1:
+                weighted = x0_stage[:, 0 : 2 * S].bitcast(F32)
             else:
                 weighted = cosine[s][:]
             nc.vector.tensor_tensor(out=weighted, in0=cosine[s][:], in1=wgs_of[i], op=ALU.mult)
-            nc.vector.tensor_tensor(out=pages[s][:].indirect(place[:]), in0=turns[s][:], in1=weighted, op=ALU.mult)
+            nc.vector.tensor_tensor(out=pages[s][:].indirect(place[:]), in0=larger, in1=weighted, op=ALU.mult)
             if s == 0:
-                quantise(w1_q[0, 1], w1_raw[0, 1], w1_stage, True, 1, PACK)
+                quantise(w1_q[0, 1], w1_raw[0, 1], w1_first_stage[:, 2 * S :], True, 1, PACK)
             if s + 1 == PACK:
                 cosine_of(s + 1)
                 reach_of(s + 1)
@@ -338,9 +355,9 @@ def tile_list_proximity_limit_features_kernel(
             second_stage(c, 1, x_codes[:], x_plane[:])
         for c in range(CHUNKS):
             cols = slice(c * CHUNK, (c + 1) * CHUNK)
-            y2 = ring.tile([P, N_TILES * CHUNK], F32, name="y2")
+            y2 = ring.tile([P, N_TILES * CHUNK], F32, name="cosine")
             nc.scalar.copy(out=y2[:], in_=y_banks[c][1][:, 0 : N_TILES * CHUNK])
-            res = ring.tile([P, N_TILES, CHUNK], F32, name="res")
+            res = ring.tile([P, N_TILES, CHUNK], F32, name="turns")
             for n in range(N_TILES):
                 nc.vector.scalar_tensor_tensor(
                     out=res[:, n, :], in0=y_banks[c][0][:, n * CHUNK : (n + 1) * CHUNK], scalar=margin_sb[:, n : n + 1],

import math
from contextlib import ExitStack

import concourse.mybir as mybir
from concourse.masks import make_identity

K, H, N, T, S, T2, M = 1024, 1024, 384, 2048, 512, 1024, 512
FLOPS = 2 * 3 * K * H * S + 2 * 2 * H * N * M

F32 = mybir.dt.float32
BF16 = mybir.dt.bfloat16
I32 = mybir.dt.int32
U32 = mybir.dt.uint32
U16 = mybir.dt.uint16
U8 = mybir.dt.uint8
FP8X4 = mybir.dt.float8_e4m3fn_x4
FP4X4 = mybir.dt.float4_e2m1fn_x4
ALU = mybir.AluOpType
ACT = mybir.ActivationFunctionType

P = 128
PACK = 4
PASS = P * PACK
PASSES = 2
SLICES = PASSES * PACK
N_TILES = N // P
CHUNKS = 4
CHUNK = M // CHUNKS
REACH_BANK = (0, 3, 1, 7, 3, 1, 7, 6)
ANGLE_BANK = (2, 3, 1, 7, 6, 3, 1, 7)
NEAR_BANK = (4, 2, 0, 5)


def tile_list_proximity_limit_features_kernel(
    tc, tab_words, tab_scales, offs, w1, w2_words, w2_scales, w3, page0, offs2, wgs,
    offs3, wgt, w4, w5_words, w5_scales, margin, out,
):
    nc = tc.nc
    with ExitStack() as ctx:
        keep = ctx.enter_context(tc.tile_pool(name="keep", bufs=1))
        ring = ctx.enter_context(tc.tile_pool(name="ring", bufs=4))
        psum = ctx.enter_context(tc.psum_pool(name="psum", bufs=1))

        def kept(shape, dtype, name):
            return keep.tile(shape, dtype, name=name, align_bytes=64)

        def load_scale_rows(queue, plane, rows):
            for q in (0, 2, 1, 3):
                queue.dma_start(
                    out=plane[32 * q : 32 * q + 4, :, :].bitcast(I32),
                    in_=rows[:, 4 * q : 4 * q + 4, :].rearrange("a r c -> r a c").bitcast(I32),
                )

        def clear(plane):
            nc.vector.memset(plane[:].rearrange("p a c -> p (a c)").bitcast(I32), 0)

        tab_plane = kept([P, PASSES, T], U8, "tab_plane")
        w2_plane_raw = kept([P, PASSES, H], U8, "w2_plane_raw")
        w5_plane = kept([P, PASSES, N], U8, "w5_plane")
        nc.gpsimd.memset(tab_plane[:, 0, :].bitcast(I32), 0)
        nc.vector.memset(tab_plane[:, 1, :].bitcast(I32), 0)
        clear(w2_plane_raw)
        clear(w5_plane)
        ident = kept([P, P], F32, "ident")
        make_identity(nc, ident[:])
        warm = kept([P, 1], F32, "warm")
        nc.scalar.activation(out=warm[:], in_=ident[:, 0:1], func=ACT.Sin)

        def load_list(dram, name):
            t = keep.tile([P, S // 16], U16, name=name)
            nc.sync.dma_start(t[:], dram)
            return t

        def load_half(w, b, a, raw=None):
            if raw is None:
                raw = ring.tile([P, PACK, PASS], F32, name="raw", bufs=3)
            nc.sync.dma_start(
                out=raw[:],
                in_=w[a * PASS : (a + 1) * PASS, b * PASS : (b + 1) * PASS].rearrange("(p j) c -> p j c", j=PACK),
            )
            return raw

        page_rows = page0.rearrange("(b p i) t -> b i p t", b=PASSES, i=PACK)

        def load_page(s):
            if s == SLICES - 1:
                t = ring.tile([P, T2], F32, name="raw", bufs=3)
            else:
                t = kept([P, T2], F32, {4: "w2_raw", 5: "tab0", 6: "tab1"}.get(s, "page%d" % s))
            nc.sync.dma_start(out=t[:], in_=page_rows[s // PACK, s % PACK])
            return t

        wgs_rows = wgs.rearrange("(q i) j -> q i j", i=PACK)

        def load_wgs(first, count, name):
            t = kept([P, count, S], F32, name)
            for q in (0, 2, 1, 3):
                nc.sync.dma_start(out=t[32 * q : 32 * q + 32, :, :], in_=wgs_rows[:, first : first + count, :])
            return t

        pick = load_list(offs, "pick")
        w2_raw = kept([P, PASSES, H // 2], I32, "w2_raw")
        nc.sync.dma_start(out=w2_raw[:], in_=w2_words.rearrange("a p c -> p a c").bitcast(I32))
        tab = [kept([P, T], I32, "tab%d" % a) for a in range(PASSES)]
        nc.sync.dma_start(out=tab[0][:], in_=tab_words[0].rearrange("p t i -> p (t i)").bitcast(I32))
        load_scale_rows(nc.sync, tab_plane, tab_scales)
        nc.sync.dma_start(out=tab[1][:], in_=tab_words[1].rearrange("p t i -> p (t i)").bitcast(I32))
        load_scale_rows(nc.sync, w2_plane_raw, w2_scales)
        first_raw = [kept([P, PACK, PASS], F32, "first_raw%d" % b) for b in range(PASSES)]
        w3_raw = {(0, 0): load_half(w3, 0, 0, first_raw[0]), (0, 1): load_half(w3, 0, 1)}
        w1_raw = {(0, a): load_half(w1, 0, a) for a in range(PASSES)}
        place = load_list(offs2, "place")
        pages = [load_page(0)]
        wgs_first = load_wgs(0, 1, "wgs_first")
        links = load_list(offs3, "links")
        wgt_sb = kept([P, M], F32, "wgt_sb")
        nc.sync.dma_start(out=wgt_sb[:], in_=wgt)
        pages.append(load_page(1))
        wgs_rest = load_wgs(1, PACK - 1, "wgs_rest")
        wgs_of = [wgs_first[:, 0, :]] + [wgs_rest[:, i, :] for i in range(PACK - 1)]

        w2_codes = kept([P, PASSES * H // 2], I32, "w2_codes")
        nc.vector.tensor_copy(
            out=w2_codes[:].bitcast(U16).rearrange("p (g t q) -> p g t q", t=PACK, q=P),
            in_=w2_raw[:].rearrange("p a c -> p (a c)").bitcast(U16).rearrange("p (g q t) -> p g t q", t=PACK, q=P),
        )
        v_codes = kept([P, PASSES, S], U32, "v_codes")
        v_plane = kept([P, PASSES, S], U8, "v_plane")
        nc.vector.tensor_copy(out=v_codes[:, 0, :], in_=tab[0][:].bitcast(U32).indirect(pick[:]))
        for a in range(PASSES):
            nc.vector.tensor_copy(out=v_plane[:, a, :], in_=tab_plane[:, a, :].indirect(pick[:]))
        nc.vector.tensor_copy(out=v_codes[:, 1, :], in_=tab[1][:].bitcast(U32).indirect(pick[:]))
        w2_plane = kept([P, PASSES * H], U8, "w2_plane")
        nc.vector.tensor_copy(
            out=w2_plane[:].rearrange("p (g t q) -> p g t q", t=PACK, q=P),
            in_=w2_plane_raw[:].rearrange("p a (b q t) -> p (a b) t q", t=PACK, q=P),
        )

        def operand(name):
            return kept([P, PASS], U32, name + "_codes"), kept([P, PASS], U8, name + "_plane")

        def quantise(dest, raw, part, on_vector, first=0, last=PACK):
            copy = nc.vector.tensor_copy if on_vector else nc.scalar.copy
            copy(
                out=part.rearrange("p (t q j) -> p q j t", q=P, j=PACK),
                in_=raw[:].rearrange("p j (q t) -> p q j t", t=PACK)[:, :, :, first:last],
            )
            codes, plane = dest
            cols = slice(first * P, last * P)
            nc.vector.quantize_mx(out=codes[:, cols].bitcast(FP8X4), scales=plane[:, cols], in_=part)

        def stage_tile():
            return ring.tile([P, PACK * PASS], BF16, name="stage", bufs=2, align_bytes=64)

        w1_q = {(b, a): operand("w1_%d%d" % (b, a)) for b in range(PASSES) for a in range(PASSES)}
        w3_q = {(b, a): operand("w3_%d%d" % (b, a)) for b in range(PASSES) for a in range(PASSES)}
        quantise(w3_q[0, 0], w3_raw[0, 0], stage_tile()[:], True)
        w3_stage = stage_tile()
        quantise(w3_q[0, 1], w3_raw[0, 1], w3_stage[:, 0:PASS], True, 0, 1)
        quantise(w3_q[0, 1], w3_raw[0, 1], w3_stage[:, PASS:], False, 1, PACK)

        picked = [kept([P, PACK, M], F32, "picked%d" % b) for b in range(PASSES)]
        w4_stage = kept([P, PASSES * PACK * N], BF16, "w4_stage")
        w1_first_stage = kept([P, 5 * S], BF16, "w1_first_stage")
        x0_stage = kept([P, PACK * M], BF16, "x0_stage")
        second_stage_in = kept([P, 2 * PASSES, PACK * PASS], BF16, "second_half_stage")

        reach_sb, turns, cosine = {}, {}, {}
        banks = [psum.tile([P, S], F32, name="bank%d" % n) for n in range(8)]

        def reach_of(s):
            b, i = divmod(s, PACK)
            bank = banks[REACH_BANK[s]]
            for a in range(PASSES):
                c0 = a * H + s * P
                nc.tensor.matmul_mx(
                    out=bank[:],
                    lhsT=w2_codes[:].bitcast(U8)[:, 2 * c0 : 2 * (c0 + P)].bitcast(FP4X4),
                    lhsT_scale=w2_plane[:, c0 : c0 + P],
                    rhs=v_codes[:, a, :].bitcast(FP8X4), rhs_scale=v_plane[:, a, :],
                    start=(a == 0), stop=(a == PASSES - 1),
                )
            if s in (1, 2):
                reach_sb[s] = w1_first_stage[:, (s - 1) * 3 * S : (s - 1) * 3 * S + 2 * S].bitcast(F32)
            else:
                reach_sb[s] = first_raw[b][:, (1, 0, 0, 2)[s] if b == 0 else i, :]
            nc.scalar.copy(out=reach_sb[s], in_=bank[:])

        def cosine_of(s):
            b, i = divmod(s, PACK)
            angle = banks[ANGLE_BANK[s]]
            for jb in range(S // P):
                for a in ((0, 1), (1, 0))[b]:
                    codes, plane = w3_q[b, a]
                    nc.tensor.matmul_mx(
                        out=angle[:, jb * P : (jb + 1) * P],
                        lhsT=v_codes[:, a, jb * P : (jb + 1) * P].bitcast(FP8X4),
                        lhsT_scale=v_plane[:, a, jb * P : (jb + 1) * P],
                        rhs=codes[:, i * P : (i + 1) * P].bitcast(FP8X4), rhs_scale=plane[:, i * P : (i + 1) * P],
                        start=(a == b), stop=(a != b),
                    )
            if s == SLICES - 1:
                turns[s] = kept([P, S], F32, "last")
            else:
                turns[s] = ring.tile([P, S], F32, name="turns")
            nc.scalar.activation(out=turns[s][:], in_=angle[:], func=ACT.Abs, scale=1.0 / (2.0 * math.pi))
            if s < 3:
                count = first_raw[0][:, s + 1, :].bitcast(U32)
            elif s == 3:
                count = second_stage_in[:, :, 0 : 2 * P].bitcast(U32)
            elif s == 4:
                count = first_raw[1][:].rearrange("p i c -> p (i c)")[:, 768:1280].bitcast(U32)
            elif s == 5:
                count = w4_stage[:, 1024:2048].bitcast(U32)
            elif s == 7:
                count = x0_stage[:, 0:1024].bitcast(U32)
            else:
                count = first_raw[0][:, PACK - 1, :].bitcast(U32)
            runs = PACK if s == 3 else 1
            count = count if s == 3 else count.rearrange("p (r c) -> p r c", r=runs)
            nc.scalar.activation(out=count, in_=turns[s][:].rearrange("p (r c) -> p r c", r=runs), func=ACT.Copy, bias=0.25)
            whole = first_raw[0][:, 0, :] if s == 0 else picked[(s - 1) // PACK][:, (s - 1) % PACK, :]
            nc.scalar.activation(out=whole.rearrange("p (r c) -> p r c", r=runs), in_=count, func=ACT.Copy, scale=-1.0, bias=0.25)
            frac = angle
            for term, part in enumerate((turns[s][:], whole)):
                for jb in range(S // P):
                    cols = slice(jb * P, (jb + 1) * P)
                    nc.tensor.matmul(
                        frac[:, cols], lhsT=part[:, cols], rhs=ident[:], is_transpose=True,
                        start=(term == 0 and jb == 0), stop=(term == 1 and jb == S // P - 1),
                    )
            cosine[s] = ring.tile([P, S], F32, name="cosine")
            nc.scalar.activation(out=cosine[s][:], in_=frac[:], func=ACT.Sin, scale=2.0 * math.pi)

        def gather(s, c0, c1):
            b, i = divmod(s, PACK)
            nc.vector.tensor_tensor(
                out=picked[b][:, i, c0:c1], in0=pages[s][:].indirect(links[:, c0 // 16 : c1 // 16]),
                in1=wgt_sb[:, c0:c1], op=ALU.mult,
            )

        def interleave(stage, planes, on_vector=False):
            copy = nc.vector.tensor_copy if on_vector else nc.scalar.copy
            copy(
                out=stage.rearrange("p (c i j) -> p c j i", i=4, j=PACK),
                in_=planes.rearrange("p j (c i) -> p c j i", i=4),
            )

        cosine_of(0)
        reach_of(0)
        quantise(w1_q[0, 0], w1_raw[0, 0], stage_tile()[:], True)
        quantise(w1_q[0, 1], w1_raw[0, 1], w1_first_stage[:, 768:1280], True, 0, 1)

        for a in range(PASSES):
            w1_raw[1, a] = load_half(w1, 1, a, kept([P, PACK, PASS], F32, "w1_raw%d" % a))
        pages.append(load_page(2))
        w3_raw[1, 0] = load_half(w3, 1, 0, kept([P, PACK, PASS], F32, "w3_raw"))
        w3_raw[1, 1] = load_half(w3, 1, 1, first_raw[1])
        for s in range(3, SLICES):
            pages.append(load_page(s))
        w4_raw = []
        for a in range(PASSES):
            raw = ring.tile([P, PACK, N], F32, name="raw", bufs=3)
            nc.sync.dma_start(out=raw[:], in_=w4[a * PASS : (a + 1) * PASS, :].rearrange("(p j) c -> p j c", j=PACK))
            w4_raw.append(raw)
        w5_codes = kept([P, PASSES, N], I32, "w5_codes")
        nc.sync.dma_start(out=w5_codes[:], in_=w5_words.rearrange("a p c i -> p a (c i)").bitcast(I32))
        load_scale_rows(nc.sync, w5_plane, w5_scales)
        margin_sb = kept([P, N_TILES], F32, "margin_sb")
        with nc.allow_non_contiguous_dma(reason="one margin value a partition"):
            nc.sync.dma_start(out=margin_sb[:], in_=margin.rearrange("(n p) -> p n", p=P))

        w4_codes = kept([P, PASSES, N], U32, "w4_codes")
        w4_plane = kept([P, PASSES, N], U8, "w4_plane")
        x0_codes = [kept([P, M // 2], U32, "x0_codes")]
        x0_plane = [kept([P, M // 2], U8, "x0_plane%d" % h) for h in range(2)]

        for s in range(SLICES):
            b, i = divmod(s, PACK)
            near = banks[NEAR_BANK[i]]
            order = (0, 1) if s == 0 else (1, 0)
            for a in order:
                codes, plane = w1_q[b, a]
                nc.tensor.matmul_mx(
                    out=near[:],
                    lhsT=codes[:, i * P : (i + 1) * P].bitcast(FP8X4), lhsT_scale=plane[:, i * P : (i + 1) * P],
                    rhs=v_codes[:, a, :].bitcast(FP8X4), rhs_scale=v_plane[:, a, :],
                    start=(a == order[0]), stop=(a == order[1]),
                )
            larger = {1: reach_sb[0], 2: turns[0][:]}.get(s, turns[s][:])
            nc.vector.tensor_tensor(out=larger, in0=near[:], in1=reach_sb[s], op=ALU.max)
            if s > 0:
                gather(s - 1, 0, M)
            if s == PACK - 1:
                for a in range(PASSES):
                    quantise(w1_q[1, a], w1_raw[1, a], second_stage_in[:, a, :], False)
                quantise(w3_q[1, 0], w3_raw[1, 0], second_stage_in[:, 2, 0 : 2 * PASS], False, 0, 2)
                quantise(w3_q[1, 1], w3_raw[1, 1], second_stage_in[:, 3, PASS : 3 * PASS], False, 0, 2)
                quantise(w3_q[1, 1], w3_raw[1, 1], second_stage_in[:, 2, 2 * PASS :], False, 2, PACK)
                quantise(w3_q[1, 0], w3_raw[1, 0], second_stage_in[:, 3, 2 * PASS :], False, 2, PACK)
                weighted = second_stage_in[:, 3, 0 : 2 * S].bitcast(F32)
            elif s == 0:
                weighted = reach_sb[s]
            elif s == SLICES - 1:
                weighted = x0_stage[:, 0 : 2 * S].bitcast(F32)
            else:
                weighted = cosine[s][:]
            nc.vector.tensor_tensor(out=weighted, in0=cosine[s][:], in1=wgs_of[i], op=ALU.mult)
            nc.vector.tensor_tensor(out=pages[s][:].indirect(place[:]), in0=larger, in1=weighted, op=ALU.mult)
            if s == 0:
                quantise(w1_q[0, 1], w1_raw[0, 1], w1_first_stage[:, 2 * S :], True, 1, PACK)
            if s + 1 == PACK:
                cosine_of(s + 1)
                reach_of(s + 1)
            elif s + 1 < SLICES:
                reach_of(s + 1)
                cosine_of(s + 1)
            if s == 5:
                for a in range(PASSES):
                    stage = w4_stage[:, a * PACK * N : (a + 1) * PACK * N]
                    interleave(stage, w4_raw[a][:])
                    nc.vector.quantize_mx(out=w4_codes[:, a, :].bitcast(FP8X4), scales=w4_plane[:, a, :], in_=stage)
            if s == 6:
                interleave(x0_stage[:], picked[0][:])
                nc.vector.quantize_mx(out=x0_codes[0][:].bitcast(FP8X4), scales=x0_plane[0][:], in_=x0_stage[:, 0 : 2 * M])


        weights = ((w4_codes, w4_plane), (w5_codes, w5_plane))
        y_banks = [banks[2 * c : 2 * c + 2] for c in range(CHUNKS)]

        def second_stage(c, b, x_codes, x_plane):
            for y in (1, 0):
                codes, plane = weights[y]
                for n in range(N_TILES):
                    nc.tensor.matmul_mx(
                        out=y_banks[c][y][:, n * CHUNK : (n + 1) * CHUNK],
                        lhsT=codes[:, b, n * P : (n + 1) * P].bitcast(FP8X4), lhsT_scale=plane[:, b, n * P : (n + 1) * P],
                        rhs=x_codes.bitcast(FP8X4), rhs_scale=x_plane,
                        start=(b == 0 and n == 0), stop=(b == PASSES - 1 and n == N_TILES - 1),
                    )

        x0_codes.append(kept([P, M // 2], U32, "last"))
        nc.vector.quantize_mx(out=x0_codes[1][:].bitcast(FP8X4), scales=x0_plane[1][:], in_=x0_stage[:, 2 * M :])
        for c in range(CHUNKS):
            cols = slice(c % 2 * CHUNK, (c % 2 + 1) * CHUNK)
            second_stage(c, 0, x0_codes[c // 2][:, cols], x0_plane[c // 2][:, cols])
        out_rows = out.rearrange("(n p) m -> p n m", p=P)
        for c in range(CHUNKS):
            gather(SLICES - 1, c * CHUNK, (c + 1) * CHUNK)
            stage = kept([P, PACK * CHUNK], BF16, "x1_stage%d" % c)
            interleave(stage[:], picked[1][:, :, c * CHUNK : (c + 1) * CHUNK], c == 0)
            x_codes = kept([P, CHUNK], U32, "x1_codes%d" % c)
            x_plane = kept([P, CHUNK], U8, "x1_plane%d" % c)
            nc.vector.quantize_mx(out=x_codes[:].bitcast(FP8X4), scales=x_plane[:], in_=stage[:])
            second_stage(c, 1, x_codes[:], x_plane[:])
        for c in range(CHUNKS):
            cols = slice(c * CHUNK, (c + 1) * CHUNK)
            y2 = ring.tile([P, N_TILES * CHUNK], F32, name="cosine")
            nc.scalar.copy(out=y2[:], in_=y_banks[c][1][:, 0 : N_TILES * CHUNK])
            res = ring.tile([P, N_TILES, CHUNK], F32, name="turns")
            for n in range(N_TILES):
                nc.vector.scalar_tensor_tensor(
                    out=res[:, n, :], in0=y_banks[c][0][:, n * CHUNK : (n + 1) * CHUNK], scalar=margin_sb[:, n : n + 1],
                    in1=y2[:, n * CHUNK : (n + 1) * CHUNK], op0=ALU.add, op1=ALU.mult,
                )
            nc.sync.dma_start(out=out_rows[:, :, cols], in_=res[:])
